import numpy as np
import ml_dtypes


def mxq(x, axis, fmt="e4m3"):
    dtype, down = {"e4m3": (ml_dtypes.float8_e4m3fn, 7), "e5m2": (ml_dtypes.float8_e5m2, 14)}[fmt]
    v = np.moveaxis(np.asarray(x, np.float32).astype(ml_dtypes.bfloat16).astype(np.float64), axis, -1)
    blocks = v.reshape(v.shape[:-1] + (-1, 32))
    amax = np.abs(blocks).max(-1, keepdims=True)
    byte = np.maximum(np.where(amax > 0, np.frexp(amax)[1] - 1 + 127, 0) - down, 1)
    scale = np.exp2(byte - 127.0)
    codes = (blocks / scale).astype(np.float32).astype(dtype).astype(np.float64)
    return np.moveaxis((codes * scale).reshape(v.shape), -1, axis)


WIDE = False


def mx_kscale(k):
    if not WIDE:
        return np.ones(k)
    levels = np.array([10, -10, 5, -5, 0])
    if k % 512:
        return np.exp2(np.random.permutation(np.resize(levels, k // 32))).repeat(32)
    a = np.empty((k // 512, 16))
    for p in range(k // 512):
        a[p, :8] = np.random.permutation(np.resize(levels, 8))
        for g in range(8):
            far = levels[np.abs(levels - a[p, g]) >= 10]
            a[p, g + 8] = far[np.random.randint(len(far))]
    return np.exp2(a.ravel()).repeat(32)


def f64(x):
    return np.asarray(x).astype(np.float64)


def split(x):
    m, e = np.frexp(f64(x))
    hi = np.ldexp(np.trunc(16.0 * m) / 16.0, e)
    return hi, f64(x) - hi


K, M, T = 512, 512, 1536


def setup_inputs():
    n = np.random.standard_normal
    s = mx_kscale(K)[:, None]
    return {
        "w": (n((K, M)) / np.sqrt(K) / s).astype(np.float32),
        "x": (n((K, T)) * s).astype(np.float32),
        "g": (n((1536, 512))).astype(np.float32),
    }


def reference(w, x, g):
    w_hi, w_lo = split(w)
    w_hi_, w_lo_ = mxq(w_hi, 0, "e4m3"), mxq(w_lo, 0, "e4m3")
    x_hi, x_lo = split(x)
    x_hi_, x_lo_ = mxq(x_hi, 0, "e4m3"), mxq(x_lo, 0, "e4m3")
    y = x_hi_.T @ w_hi_ + x_lo_.T @ w_hi_ + x_hi_.T @ w_lo_
    return f64(g) * y

@@ -1,0 +1,207 @@
+from contextlib import ExitStack
+
+import concourse.mybir as mybir
+
+K, N, T = 512, 512, 1536
+FLOPS = 2 * K * N * T * 3
+
+F32 = mybir.dt.float32
+BF16 = mybir.dt.bfloat16
+I32 = mybir.dt.int32
+U32 = mybir.dt.uint32
+U8 = mybir.dt.uint8
+FP8X4 = mybir.dt.float8_e4m3fn_x4
+ALU = mybir.AluOpType
+
+P = 128
+PACK = 4
+W = 256
+MASK2 = -983056
+SI = 4
+VI = 2
+
+
+def tile_mix_split3_tm_mul_kernel(tc, w, x, g, out):
+    nc = tc.nc
+    with ExitStack() as ctx:
+        keep = ctx.enter_context(tc.tile_pool(name="keep", bufs=1))
+        psum = ctx.enter_context(tc.psum_pool(name="psum", bufs=8))
+        ctx.enter_context(tc.manual_schedule())
+
+        def load_k(src, c0, width, name):
+            raw = keep.tile([P, PACK, width], F32, name=name, align_bytes=64)
+            nc.sync.dma_start(out=raw[:], in_=src[:, c0 : c0 + width].rearrange("(p j) c -> p j c", j=PACK))
+            return raw
+
+        def load_g(c):
+            t = keep.tile([P, 4, N], F32, name="g%d" % c, align_bytes=64)
+            nc.sync.dma_start(out=t[:], in_=g[512 * c : 512 * c + 512, :].rearrange("(a p) n -> p a n", p=P))
+            return t
+
+        raws = {}
+        gs = []
+        x0 = load_k(x, 0, 256, "rx0")
+        raws["x", 0] = x0[:]
+        rw = load_k(w, 0, 512, "rw")
+        raws["w", 0] = rw[:, :, 0:256]
+        raws["w", 1] = rw[:, :, 256:512]
+        x1 = load_k(x, 256, 256, "rx1")
+        raws["x", 1] = x1[:]
+        gs.append(load_g(0))
+        x2 = load_k(x, 512, 512, "rx2")
+        raws["x", 2] = x2[:, :, 0:256]
+        raws["x", 3] = x2[:, :, 256:512]
+        gs.append(load_g(1))
+        x4 = load_k(x, 1024, 512, "rx4")
+        raws["x", 4] = x4[:, :, 0:256]
+        raws["x", 5] = x4[:, :, 256:512]
+        gs.append(load_g(2))
+
+        blocks = [("x", 0), ("w", 0), ("w", 1), ("x", 1), ("x", 2), ("x", 3), ("x", 4), ("x", 5)]
+        wq = {}
+        for part in ("hi", "lo"):
+            codes = keep.tile([P, N], U32, name="wc" + part, align_bytes=64)
+            scales = keep.tile([P, N], U8, name="ws" + part, align_bytes=64)
+            wq[part] = (codes, scales)
+        xq = {}
+        top, hi, lo = {}, {}, {}
+        for b in blocks:
+            tag = "%s%d" % b
+            top[b] = keep.tile([P, W * PACK], BF16, name="top" + tag, align_bytes=64)
+            hi[b] = keep.tile([P, W * PACK], BF16, name="hi" + tag, align_bytes=64)
+            lo[b] = keep.tile([P, W * PACK], BF16, name="lo" + tag, align_bytes=64)
+            if b[0] == "x":
+                for part in ("hi", "lo"):
+                    codes = keep.tile([P, W], U32, name="xc" + part + tag, align_bytes=64)
+                    scales = keep.tile([P, W], U8, name="xs" + part + tag, align_bytes=64)
+                    xq[b[1], part] = (codes, scales)
+
+        def grouped(t, i, c0, c1):
+            return t[:, PACK * c0 : PACK * c1].rearrange("p (c i j) -> p c j i", i=i, j=PACK)
+
+        def copy_top(b, c0=0, c1=W, eng=None):
+            src = raws[b][:, :, c0:c1].bitcast(BF16)[:, :, 1::2]
+            src = src.rearrange("p j (c i) -> p c j i", i=SI)
+            if eng is None:
+                nc.scalar.copy(out=grouped(top[b], SI, c0, c1), in_=src)
+            else:
+                nc.vector.tensor_copy(out=grouped(top[b], SI, c0, c1), in_=src)
+
+        def mask(b, c0=0, c1=W):
+            nc.vector.tensor_scalar(
+                out=hi[b][:, PACK * c0 : PACK * c1].bitcast(I32),
+                in0=top[b][:, PACK * c0 : PACK * c1].bitcast(I32),
+                scalar1=MASK2,
+                scalar2=None,
+                op0=ALU.bitwise_and,
+            )
+
+        def sub(b, c0=0, c1=W):
+            nc.vector.tensor_tensor(
+                out=grouped(lo[b], VI, c0, c1),
+                in0=raws[b][:, :, c0:c1].rearrange("p j (c i) -> p c j i", i=VI),
+                in1=grouped(hi[b], VI, c0, c1),
+                op=ALU.subtract,
+            )
+
+        def quant(b, part, c0=0, c1=W):
+            src = (hi if part == "hi" else lo)[b]
+            if b[0] == "w":
+                codes, scales = wq[part]
+                d0 = W * b[1]
+            else:
+                codes, scales = xq[b[1], part]
+                d0 = 0
+            nc.vector.quantize_mx(
+                out=codes[:, d0 + c0 : d0 + c1].bitcast(FP8X4),
+                scales=scales[:, d0 + c0 : d0 + c1],
+                in_=src[:, PACK * c0 : PACK * c1],
+            )
+
+        acc = {}
+
+        def mm(xb, h, xp, wp, start, stop):
+            codes, scales = xq[xb, xp]
+            wc, ws = wq[wp]
+            nc.tensor.matmul_mx(
+                out=acc[xb, h][:],
+                lhsT=codes[:, 128 * h : 128 * h + 128].bitcast(FP8X4),
+                lhsT_scale=scales[:, 128 * h : 128 * h + 128],
+                rhs=wc[:].bitcast(FP8X4),
+                rhs_scale=ws[:],
+                start=start,
+                stop=stop,
+            )
+
+        def mm_hi(xb):
+            for h in range(2):
+                acc[xb, h] = psum.tile([P, N], F32, name="acc")
+            for h in range(2):
+                mm(xb, h, "hi", "hi", True, False)
+            for h in range(2):
+                mm(xb, h, "hi", "lo", False, False)
+
+        def mm_lo(xb, halves=(0, 1)):
+            for h in halves:
+                mm(xb, h, "lo", "hi", False, True)
+
+        def epilogue(xb, halves=(0, 1)):
+            if (xb, "o") not in acc:
+                acc[xb, "o"] = keep.tile([P, 2, N], F32, name="o%d" % xb, align_bytes=64)
+            o = acc[xb, "o"]
+            dst = out[256 * xb : 256 * xb + 256, :].rearrange("(a p) n -> p a n", p=P)
+            for h in halves:
+                nc.vector.tensor_tensor(
+                    out=o[:, h, :],
+                    in0=acc[xb, h][:],
+                    in1=gs[xb // 2][:, 2 * (xb % 2) + h, :],
+                    op=ALU.mult,
+                )
+            h0, h1 = halves[0], halves[-1] + 1
+            nc.sync.dma_start(out=dst[:, h0:h1, :], in_=o[:, h0:h1, :])
+
+        b0 = blocks[0]
+        copy_top(b0, 0, 128)
+        copy_top(b0, 128, 256)
+        for b in blocks[1:]:
+            copy_top(b)
+        mask(b0, 0, 128)
+        mask(b0, 128, 256)
+        ready = []
+        for b, following in zip(blocks, blocks[1:]):
+            if b == b0:
+                sub(b, 0, 128)
+                quant(b, "hi")
+                sub(b, 128, 256)
+            else:
+                quant(b, "hi")
+                sub(b)
+            xb = b[1] if b[0] == "x" and b != b0 else None
+            if xb is not None:
+                mm_hi(xb)
+            mask(following)
+            quant(b, "lo")
+            if b == ("w", 1):
+                xb = 0
+                mm_hi(xb)
+            if xb is not None:
+                mm_lo(xb)
+            if ready:
+                epilogue(ready.pop(0))
+            if xb is not None:
+                ready.append(xb)
+
+        b = blocks[-1]
+        quant(b, "hi")
+        mm_hi(b[1])
+        sub(b, 0, 128)
+        sub(b, 128, 256)
+        quant(b, "lo", 0, 128)
+        mm_lo(b[1], (0,))
+        prev = ready.pop(0)
+        epilogue(prev, (0,))
+        quant(b, "lo", 128, 256)
+        mm_lo(b[1], (1,))
+        epilogue(prev, (1,))
+        epilogue(b[1], (0,))
+        epilogue(b[1], (1,))

@@ -17,8 +17,7 @@ P = 128
 PACK = 4
 W = 256
 MASK2 = -983056
-SI = 4
-VI = 2
+GP = {}
 
 
 def tile_mix_split3_tm_mul_kernel(tc, w, x, g, out):
@@ -28,42 +27,38 @@ def tile_mix_split3_tm_mul_kernel(tc, w, x, g, out):
         psum = ctx.enter_context(tc.psum_pool(name="psum", bufs=8))
         ctx.enter_context(tc.manual_schedule())
 
-        def load_k(src, c0, width, name):
-            raw = keep.tile([P, PACK, width], F32, name=name, align_bytes=64)
-            nc.sync.dma_start(out=raw[:], in_=src[:, c0 : c0 + width].rearrange("(p j) c -> p j c", j=PACK))
-            return raw
-
-        def load_g(c):
-            t = keep.tile([P, 4, N], F32, name="g%d" % c, align_bytes=64)
-            nc.sync.dma_start(out=t[:], in_=g[512 * c : 512 * c + 512, :].rearrange("(a p) n -> p a n", p=P))
-            return t
-
         raws = {}
-        gs = []
-        x0 = load_k(x, 0, 256, "rx0")
-        raws["x", 0] = x0[:]
-        rw = load_k(w, 0, 512, "rw")
-        raws["w", 0] = rw[:, :, 0:256]
-        raws["w", 1] = rw[:, :, 256:512]
-        x1 = load_k(x, 256, 256, "rx1")
-        raws["x", 1] = x1[:]
-        gs.append(load_g(0))
-        x2 = load_k(x, 512, 512, "rx2")
-        raws["x", 2] = x2[:, :, 0:256]
-        raws["x", 3] = x2[:, :, 256:512]
-        gs.append(load_g(1))
-        x4 = load_k(x, 1024, 512, "rx4")
-        raws["x", 4] = x4[:, :, 0:256]
-        raws["x", 5] = x4[:, :, 256:512]
-        gs.append(load_g(2))
+        gs = {}
+
+        def load_k(src, kind, c0, width):
+            raw = keep.tile([P, PACK, width], F32, name="r%s%d" % (kind, c0), align_bytes=64)
+            nc.sync.dma_start(out=raw[:], in_=src[:, c0 : c0 + width].rearrange("(p j) c -> p j c", j=PACK))
+            for c in range(0, width, 128):
+                raws[kind, c0 + c] = (raw, c)
+
+        def load_g(b0, blocks):
+            t = keep.tile([P, blocks, 2, N], F32, name="g%d" % b0, align_bytes=64)
+            src = g[W * b0 : W * (b0 + blocks), :].rearrange("(b m a) n -> m b (a n)", m=P, a=2)
+            nc.sync.dma_start(out=t[:].rearrange("p b a n -> p b (a n)"), in_=src)
+            for i in range(blocks):
+                gs[b0 + i] = t[:, i, :, :]
+
+        load_k(x, "x", 0, 128)
+        load_k(x, "x", 128, 128)
+        load_k(w, "w", 0, 512)
+        load_k(x, "x", 256, 256)
+        load_g(0, 1)
+        load_k(x, "x", 512, 512)
+        load_g(1, 2)
+        load_k(x, "x", 1024, 512)
+        load_g(3, 2)
+        load_g(5, 1)
 
         blocks = [("x", 0), ("w", 0), ("w", 1), ("x", 1), ("x", 2), ("x", 3), ("x", 4), ("x", 5)]
-        wq = {}
+        codes, scales = {}, {}
         for part in ("hi", "lo"):
-            codes = keep.tile([P, N], U32, name="wc" + part, align_bytes=64)
-            scales = keep.tile([P, N], U8, name="ws" + part, align_bytes=64)
-            wq[part] = (codes, scales)
-        xq = {}
+            codes["w", part] = keep.tile([P, N], U32, name="wc" + part, align_bytes=64)
+            scales["w", part] = keep.tile([P, N], U8, name="ws" + part, align_bytes=64)
         top, hi, lo = {}, {}, {}
         for b in blocks:
             tag = "%s%d" % b
@@ -72,136 +67,128 @@ def tile_mix_split3_tm_mul_kernel(tc, w, x, g, out):
             lo[b] = keep.tile([P, W * PACK], BF16, name="lo" + tag, align_bytes=64)
             if b[0] == "x":
                 for part in ("hi", "lo"):
-                    codes = keep.tile([P, W], U32, name="xc" + part + tag, align_bytes=64)
-                    scales = keep.tile([P, W], U8, name="xs" + part + tag, align_bytes=64)
-                    xq[b[1], part] = (codes, scales)
+                    codes[b, part] = keep.tile([P, W], U32, name="xc" + part + tag, align_bytes=64)
+                    scales[b, part] = keep.tile([P, W], U8, name="xs" + part + tag, align_bytes=64)
 
-        def grouped(t, i, c0, c1):
-            return t[:, PACK * c0 : PACK * c1].rearrange("p (c i j) -> p c j i", i=i, j=PACK)
+        def raw_cols(b, m0, m1):
+            raw, c = raws[b[0], W * b[1] + (2 * m0) // 128 * 128]
+            c = c + 2 * m0 % 128
+            return raw[:, :, c : c + 2 * (m1 - m0)]
 
-        def copy_top(b, c0=0, c1=W, eng=None):
-            src = raws[b][:, :, c0:c1].bitcast(BF16)[:, :, 1::2]
-            src = src.rearrange("p j (c i) -> p c j i", i=SI)
-            if eng is None:
-                nc.scalar.copy(out=grouped(top[b], SI, c0, c1), in_=src)
-            else:
-                nc.vector.tensor_copy(out=grouped(top[b], SI, c0, c1), in_=src)
+        def pairs(t, b, m0, m1):
+            if b[0] == "w":
+                return t[:].rearrange("p (m a j) -> p m j a", a=2, j=PACK)[:, m0:m1]
+            return t[:].rearrange("p (a m j) -> p m j a", a=2, j=PACK)[:, m0:m1]
 
-        def mask(b, c0=0, c1=W):
-            nc.vector.tensor_scalar(
-                out=hi[b][:, PACK * c0 : PACK * c1].bitcast(I32),
-                in0=top[b][:, PACK * c0 : PACK * c1].bitcast(I32),
-                scalar1=MASK2,
-                scalar2=None,
-                op0=ALU.bitwise_and,
-            )
+        def copy_top(b, m0=0, m1=128):
+            src = raw_cols(b, m0, m1).bitcast(BF16)[:, :, 1::2]
+            nc.scalar.copy(out=pairs(top[b], b, m0, m1), in_=src.rearrange("p j (m a) -> p m j a", a=2))
 
-        def sub(b, c0=0, c1=W):
-            nc.vector.tensor_tensor(
-                out=grouped(lo[b], VI, c0, c1),
-                in0=raws[b][:, :, c0:c1].rearrange("p j (c i) -> p c j i", i=VI),
-                in1=grouped(hi[b], VI, c0, c1),
+        def mask(b, m0=0, m1=128):
+            view = [
+                t[b][:].bitcast(I32).rearrange("p (a f) -> p a f", a=2)[:, :, 2 * m0 : 2 * m1] for t in (hi, top)
+            ]
+            nc.vector.tensor_scalar(out=view[0], in0=view[1], scalar1=MASK2, scalar2=None, op0=ALU.bitwise_and)
+
+        def sub(b, m0=0, m1=128, eng=None):
+            (nc.vector if eng is None else eng).tensor_tensor(
+                out=pairs(lo[b], b, m0, m1),
+                in0=raw_cols(b, m0, m1).rearrange("p j (m a) -> p m j a", a=2),
+                in1=pairs(hi[b], b, m0, m1),
                 op=ALU.subtract,
             )
 
         def quant(b, part, c0=0, c1=W):
             src = (hi if part == "hi" else lo)[b]
-            if b[0] == "w":
-                codes, scales = wq[part]
-                d0 = W * b[1]
-            else:
-                codes, scales = xq[b[1], part]
-                d0 = 0
+            key, d0 = ("w", W * b[1]) if b[0] == "w" else (b, 0)
             nc.vector.quantize_mx(
-                out=codes[:, d0 + c0 : d0 + c1].bitcast(FP8X4),
-                scales=scales[:, d0 + c0 : d0 + c1],
+                out=codes[key, part][:, d0 + c0 : d0 + c1].bitcast(FP8X4),
+                scales=scales[key, part][:, d0 + c0 : d0 + c1],
                 in_=src[:, PACK * c0 : PACK * c1],
             )
 
-        acc = {}
+        acc, outs = {}, {}
 
-        def mm(xb, h, xp, wp, start, stop):
-            codes, scales = xq[xb, xp]
-            wc, ws = wq[wp]
+        def mm(xb, a, xp, wp, start, stop):
+            cols = slice(128 * a, 128 * a + 128)
             nc.tensor.matmul_mx(
-                out=acc[xb, h][:],
-                lhsT=codes[:, 128 * h : 128 * h + 128].bitcast(FP8X4),
-                lhsT_scale=scales[:, 128 * h : 128 * h + 128],
-                rhs=wc[:].bitcast(FP8X4),
-                rhs_scale=ws[:],
+                out=acc[xb, a][:],
+                lhsT=codes[("x", xb), xp][:, cols].bitcast(FP8X4),
+                lhsT_scale=scales[("x", xb), xp][:, cols],
+                rhs=codes["w", wp][:].bitcast(FP8X4),
+                rhs_scale=scales["w", wp][:],
                 start=start,
                 stop=stop,
             )
 
         def mm_hi(xb):
-            for h in range(2):
-                acc[xb, h] = psum.tile([P, N], F32, name="acc")
-            for h in range(2):
-                mm(xb, h, "hi", "hi", True, False)
-            for h in range(2):
-                mm(xb, h, "hi", "lo", False, False)
+            for a in range(2):
+                acc[xb, a] = psum.tile([P, N], F32, name="acc")
+                mm(xb, a, "hi", "hi", True, False)
+                mm(xb, a, "hi", "lo", False, False)
 
         def mm_lo(xb, halves=(0, 1)):
-            for h in halves:
-                mm(xb, h, "lo", "hi", False, True)
+            for a in halves:
+                mm(xb, a, "lo", "hi", False, True)
 
-        def epilogue(xb, halves=(0, 1)):
-            if (xb, "o") not in acc:
-                acc[xb, "o"] = keep.tile([P, 2, N], F32, name="o%d" % xb, align_bytes=64)
-            o = acc[xb, "o"]
-            dst = out[256 * xb : 256 * xb + 256, :].rearrange("(a p) n -> p a n", p=P)
-            for h in halves:
-                nc.vector.tensor_tensor(
-                    out=o[:, h, :],
-                    in0=acc[xb, h][:],
-                    in1=gs[xb // 2][:, 2 * (xb % 2) + h, :],
-                    op=ALU.mult,
-                )
-            h0, h1 = halves[0], halves[-1] + 1
-            nc.sync.dma_start(out=dst[:, h0:h1, :], in_=o[:, h0:h1, :])
+        def epilogue(xb, a):
+            if a == 0:
+                outs[xb] = keep.tile([P, 2, N], F32, name="o%d" % xb, align_bytes=64)
+            nc.vector.tensor_tensor(out=outs[xb][:, a, :], in0=acc[xb, a][:], in1=gs[xb][:, a, :], op=ALU.mult)
 
-        b0 = blocks[0]
-        copy_top(b0, 0, 128)
-        copy_top(b0, 128, 256)
+        def store(xb, a=None):
+            dst = out[W * xb : W * xb + W, :].rearrange("(m a) n -> m a n", a=2)
+            if a is None:
+                nc.sync.dma_start(out=dst.rearrange("m a n -> m (a n)"), in_=outs[xb][:].rearrange("p a n -> p (a n)"))
+            else:
+                nc.sync.dma_start(out=dst[:, a, :], in_=outs[xb][:, a, :])
+
+        first = blocks[0]
+        copy_top(first, 0, 64)
+        copy_top(first, 64, 128)
         for b in blocks[1:]:
             copy_top(b)
-        mask(b0, 0, 128)
-        mask(b0, 128, 256)
-        ready = []
+
+        mask(first, 0, 64)
+        sub(first, 0, 64)
+        mask(first, 64, 128)
+        sub(first, 64, 128)
+        prev = None
         for b, following in zip(blocks, blocks[1:]):
-            if b == b0:
-                sub(b, 0, 128)
-                quant(b, "hi")
-                sub(b, 128, 256)
-            else:
-                quant(b, "hi")
+            quant(b, "hi")
+            if b != first:
                 sub(b)
-            xb = b[1] if b[0] == "x" and b != b0 else None
+            xb = b[1] if b[0] == "x" and b != first else None
             if xb is not None:
                 mm_hi(xb)
-            mask(following)
-            quant(b, "lo")
+            if prev is None:
+                mask(following)
+                quant(b, "lo")
+            else:
+                epilogue(prev, 0)
+                quant(b, "lo")
+                mask(following)
+                epilogue(prev, 1)
+                store(prev)
             if b == ("w", 1):
                 xb = 0
                 mm_hi(xb)
             if xb is not None:
                 mm_lo(xb)
-            if ready:
-                epilogue(ready.pop(0))
-            if xb is not None:
-                ready.append(xb)
+                prev = xb
 
         b = blocks[-1]
         quant(b, "hi")
         mm_hi(b[1])
-        sub(b, 0, 128)
-        sub(b, 128, 256)
+        sub(b, 0, 64)
+        sub(b, 64, 128)
+        epilogue(prev, 0)
         quant(b, "lo", 0, 128)
         mm_lo(b[1], (0,))
-        prev = ready.pop(0)
-        epilogue(prev, (0,))
         quant(b, "lo", 128, 256)
         mm_lo(b[1], (1,))
-        epilogue(prev, (1,))
-        epilogue(b[1], (0,))
-        epilogue(b[1], (1,))
+        epilogue(prev, 1)
+        store(prev)
+        for a in range(2):
+            epilogue(b[1], a)
+            store(b[1], a)

@@ -17,7 +17,6 @@ P = 128
 PACK = 4
 W = 256
 MASK2 = -983056
-GP = {}
 
 
 def tile_mix_split3_tm_mul_kernel(tc, w, x, g, out):
@@ -27,34 +26,37 @@ def tile_mix_split3_tm_mul_kernel(tc, w, x, g, out):
         psum = ctx.enter_context(tc.psum_pool(name="psum", bufs=8))
         ctx.enter_context(tc.manual_schedule())
 
-        raws = {}
+        loaded = []
         gs = {}
+
+        def raw_cols(b, c0, c1):
+            for kind, d0, d1, raw in loaded:
+                if kind == b[0] and d0 <= W * b[1] + c0 and W * b[1] + c1 <= d1:
+                    s0 = W * b[1] + c0 - d0
+                    return raw[:, :, s0 : s0 + c1 - c0]
+            raise ValueError("columns not loaded in one piece")
 
         def load_k(src, kind, c0, width):
             raw = keep.tile([P, PACK, width], F32, name="r%s%d" % (kind, c0), align_bytes=64)
             nc.sync.dma_start(out=raw[:], in_=src[:, c0 : c0 + width].rearrange("(p j) c -> p j c", j=PACK))
-            for c in range(0, width, 128):
-                raws[kind, c0 + c] = (raw, c)
+            loaded.append((kind, c0, c0 + width, raw))
 
-        def load_g(b0, blocks):
-            t = keep.tile([P, blocks, 2, N], F32, name="g%d" % b0, align_bytes=64)
-            src = g[W * b0 : W * (b0 + blocks), :].rearrange("(b m a) n -> m b (a n)", m=P, a=2)
-            nc.sync.dma_start(out=t[:].rearrange("p b a n -> p b (a n)"), in_=src)
-            for i in range(blocks):
-                gs[b0 + i] = t[:, i, :, :]
+        def load_g(t0, rows):
+            t = keep.tile([P, rows // P, N], F32, name="g%d" % t0, align_bytes=64)
+            nc.sync.dma_start(out=t[:], in_=g[t0 : t0 + rows, :].rearrange("(a p) n -> p a n", p=P))
+            for i in range(rows // P):
+                gs[t0 // P + i] = t[:, i, :]
 
-        load_k(x, "x", 0, 128)
-        load_k(x, "x", 128, 128)
+        load_k(x, "x", 0, 160)
+        load_k(x, "x", 160, 352)
         load_k(w, "w", 0, 512)
-        load_k(x, "x", 256, 256)
-        load_g(0, 1)
         load_k(x, "x", 512, 512)
-        load_g(1, 2)
+        load_g(0, 512)
         load_k(x, "x", 1024, 512)
-        load_g(3, 2)
-        load_g(5, 1)
+        load_g(512, 512)
+        load_g(1024, 512)
 
-        blocks = [("x", 0), ("w", 0), ("w", 1), ("x", 1), ("x", 2), ("x", 3), ("x", 4), ("x", 5)]
+        blocks = [("x", 0), ("x", 1), ("w", 0), ("w", 1), ("x", 2), ("x", 3), ("x", 4), ("x", 5)]
         codes, scales = {}, {}
         for part in ("hi", "lo"):
             codes["w", part] = keep.tile([P, N], U32, name="wc" + part, align_bytes=64)
@@ -70,31 +72,27 @@ def tile_mix_split3_tm_mul_kernel(tc, w, x, g, out):
                     codes[b, part] = keep.tile([P, W], U32, name="xc" + part + tag, align_bytes=64)
                     scales[b, part] = keep.tile([P, W], U8, name="xs" + part + tag, align_bytes=64)
 
-        def raw_cols(b, m0, m1):
-            raw, c = raws[b[0], W * b[1] + (2 * m0) // 128 * 128]
-            c = c + 2 * m0 % 128
-            return raw[:, :, c : c + 2 * (m1 - m0)]
+        def grouped(t, i, c0, c1):
+            return t[:, PACK * c0 : PACK * c1].rearrange("p (c i j) -> p c j i", i=i, j=PACK)
 
-        def pairs(t, b, m0, m1):
-            if b[0] == "w":
-                return t[:].rearrange("p (m a j) -> p m j a", a=2, j=PACK)[:, m0:m1]
-            return t[:].rearrange("p (a m j) -> p m j a", a=2, j=PACK)[:, m0:m1]
+        def copy_top(b, c0=0, c1=W):
+            src = raw_cols(b, c0, c1).bitcast(BF16)[:, :, 1::2]
+            nc.scalar.copy(out=grouped(top[b], 4, c0, c1), in_=src.rearrange("p j (c i) -> p c j i", i=4))
 
-        def copy_top(b, m0=0, m1=128):
-            src = raw_cols(b, m0, m1).bitcast(BF16)[:, :, 1::2]
-            nc.scalar.copy(out=pairs(top[b], b, m0, m1), in_=src.rearrange("p j (m a) -> p m j a", a=2))
+        def mask(b, c0=0, c1=W):
+            nc.vector.tensor_scalar(
+                out=hi[b][:, PACK * c0 : PACK * c1].bitcast(I32),
+                in0=top[b][:, PACK * c0 : PACK * c1].bitcast(I32),
+                scalar1=MASK2,
+                scalar2=None,
+                op0=ALU.bitwise_and,
+            )
 
-        def mask(b, m0=0, m1=128):
-            view = [
-                t[b][:].bitcast(I32).rearrange("p (a f) -> p a f", a=2)[:, :, 2 * m0 : 2 * m1] for t in (hi, top)
-            ]
-            nc.vector.tensor_scalar(out=view[0], in0=view[1], scalar1=MASK2, scalar2=None, op0=ALU.bitwise_and)
-
-        def sub(b, m0=0, m1=128, eng=None):
+        def sub(b, c0=0, c1=W, eng=None):
             (nc.vector if eng is None else eng).tensor_tensor(
-                out=pairs(lo[b], b, m0, m1),
-                in0=raw_cols(b, m0, m1).rearrange("p j (m a) -> p m j a", a=2),
-                in1=pairs(hi[b], b, m0, m1),
+                out=grouped(lo[b], 2, c0, c1),
+                in0=raw_cols(b, c0, c1).rearrange("p j (c i) -> p c j i", i=2),
+                in1=grouped(hi[b], 2, c0, c1),
                 op=ALU.subtract,
             )
 
@@ -109,86 +107,93 @@ def tile_mix_split3_tm_mul_kernel(tc, w, x, g, out):
 
         acc, outs = {}, {}
 
-        def mm(xb, a, xp, wp, start, stop):
-            cols = slice(128 * a, 128 * a + 128)
+        def mm(t, xp, wp, start, stop):
+            cols = slice(128 * (t % 2), 128 * (t % 2) + 128)
+            b = ("x", t // 2)
             nc.tensor.matmul_mx(
-                out=acc[xb, a][:],
-                lhsT=codes[("x", xb), xp][:, cols].bitcast(FP8X4),
-                lhsT_scale=scales[("x", xb), xp][:, cols],
+                out=acc[t][:],
+                lhsT=codes[b, xp][:, cols].bitcast(FP8X4),
+                lhsT_scale=scales[b, xp][:, cols],
                 rhs=codes["w", wp][:].bitcast(FP8X4),
                 rhs_scale=scales["w", wp][:],
                 start=start,
                 stop=stop,
             )
 
-        def mm_hi(xb):
-            for a in range(2):
-                acc[xb, a] = psum.tile([P, N], F32, name="acc")
-                mm(xb, a, "hi", "hi", True, False)
-                mm(xb, a, "hi", "lo", False, False)
+        def mm_hi(t):
+            acc[t] = psum.tile([P, N], F32, name="acc")
+            mm(t, "hi", "hi", True, False)
+            mm(t, "hi", "lo", False, False)
 
-        def mm_lo(xb, halves=(0, 1)):
-            for a in halves:
-                mm(xb, a, "lo", "hi", False, True)
+        def mm_lo(t):
+            mm(t, "lo", "hi", False, True)
 
-        def epilogue(xb, a):
-            if a == 0:
-                outs[xb] = keep.tile([P, 2, N], F32, name="o%d" % xb, align_bytes=64)
-            nc.vector.tensor_tensor(out=outs[xb][:, a, :], in0=acc[xb, a][:], in1=gs[xb][:, a, :], op=ALU.mult)
+        def epi(t, n0=0, n1=N):
+            if t // 2 not in outs:
+                outs[t // 2] = keep.tile([P, 2, N], F32, name="o%d" % (t // 2), align_bytes=64)
+            nc.vector.tensor_tensor(
+                out=outs[t // 2][:, t % 2, n0:n1], in0=acc[t][:, n0:n1], in1=gs[t][:, n0:n1], op=ALU.mult
+            )
 
-        def store(xb, a=None):
-            dst = out[W * xb : W * xb + W, :].rearrange("(m a) n -> m a n", a=2)
-            if a is None:
-                nc.sync.dma_start(out=dst.rearrange("m a n -> m (a n)"), in_=outs[xb][:].rearrange("p a n -> p (a n)"))
-            else:
-                nc.sync.dma_start(out=dst[:, a, :], in_=outs[xb][:, a, :])
+        def store(t0, t1, n0=0, n1=N):
+            dst = out[P * t0 : P * t1, n0:n1].rearrange("(a p) n -> p a n", p=P)
+            nc.sync.dma_start(out=dst, in_=outs[t0 // 2][:, t0 % 2 : t0 % 2 + t1 - t0, n0:n1])
 
+        pieces = ((0, 80), (80, 160), (160, 256))
         first = blocks[0]
-        copy_top(first, 0, 64)
-        copy_top(first, 64, 128)
+        for c0, c1 in pieces:
+            copy_top(first, c0, c1)
         for b in blocks[1:]:
             copy_top(b)
+        for c0, c1 in pieces:
+            mask(first, c0, c1)
+            sub(first, c0, c1)
 
-        mask(first, 0, 64)
-        sub(first, 0, 64)
-        mask(first, 64, 128)
-        sub(first, 64, 128)
-        prev = None
+        gp = {("x", 3): 80, ("x", 4): 120, ("x", 5): 120}
+        epis = {("x", 2): (0, 1,), ("x", 3): (2, 3, 4,), ("x", 4): (5, 6, 7,)}
         for b, following in zip(blocks, blocks[1:]):
-            quant(b, "hi")
-            if b != first:
-                sub(b)
-            xb = b[1] if b[0] == "x" and b != first else None
-            if xb is not None:
-                mm_hi(xb)
-            if prev is None:
+            if b not in epis:
+                quant(b, "hi")
+                if b != first:
+                    sub(b)
                 mask(following)
                 quant(b, "lo")
             else:
-                epilogue(prev, 0)
+                sub(b, 0, W - gp.get(b, 0))
+                quant(b, "hi")
                 quant(b, "lo")
                 mask(following)
-                epilogue(prev, 1)
-                store(prev)
+                if following in gp:
+                    sub(following, W - gp[following], W, nc.gpsimd)
             if b == ("w", 1):
-                xb = 0
-                mm_hi(xb)
-            if xb is not None:
-                mm_lo(xb)
-                prev = xb
+                for t in range(4):
+                    mm_hi(t)
+                    mm_lo(t)
+            if b[0] == "x" and b[1] >= 2:
+                for t in (2 * b[1], 2 * b[1] + 1):
+                    mm_hi(t)
+                for t in (2 * b[1], 2 * b[1] + 1):
+                    mm_lo(t)
+            for t in epis.get(b, ()):
+                epi(t)
+                if t % 2 == 1:
+                    store(t - 1, t + 1)
 
         b = blocks[-1]
         quant(b, "hi")
-        mm_hi(b[1])
-        sub(b, 0, 64)
-        sub(b, 64, 128)
-        epilogue(prev, 0)
+        mm_hi(10)
+        mm_hi(11)
+        sub(b, 0, W - gp.get(b, 0))
+        epi(8)
+        store(8, 9)
         quant(b, "lo", 0, 128)
-        mm_lo(b[1], (0,))
+        mm_lo(10)
         quant(b, "lo", 128, 256)
-        mm_lo(b[1], (1,))
-        epilogue(prev, 1)
-        store(prev)
-        for a in range(2):
-            epilogue(b[1], a)
-            store(b[1], a)
+        mm_lo(11)
+        epi(9)
+        store(9, 10)
+        epi(10)
+        store(10, 11)
+        for n0 in (0, 256):
+            epi(11, n0, n0 + 256)
+            store(11, 12, n0, n0 + 256)

@@ -15,7 +15,6 @@ ALU = mybir.AluOpType
 
 P = 128
 PACK = 4
-W = 256
 MASK2 = -983056
 
 
@@ -26,60 +25,53 @@ def tile_mix_split3_tm_mul_kernel(tc, w, x, g, out):
         psum = ctx.enter_context(tc.psum_pool(name="psum", bufs=8))
         ctx.enter_context(tc.manual_schedule())
 
-        loaded = []
-        gs = {}
+        blocks = {"xa": (x, 0, 256), "xb": (x, 256, 256), "w": (w, 0, 512), "xc": (x, 512, 512), "xd": (x, 1024, 512)}
+        top, hi, lo, codes, scales = {}, {}, {}, {}, {}
+        for b, (source, col, width) in blocks.items():
+            top[b] = keep.tile([P, width * PACK], BF16, name="top_" + b, align_bytes=64)
+            hi[b] = keep.tile([P, width * PACK], BF16, name="hi_" + b, align_bytes=64)
+            lo[b] = keep.tile([P, width * PACK], BF16, name="lo_" + b, align_bytes=64)
+            for part in ("hi", "lo"):
+                codes[b, part] = keep.tile([P, width], U32, name="codes_%s_%s" % (part, b), align_bytes=64)
+                scales[b, part] = keep.tile([P, width], U8, name="scales_%s_%s" % (part, b), align_bytes=64)
+
+        loaded, gs = [], {}
+
+        def load_k(source, c0, c1):
+            raw = keep.tile([P, PACK, c1 - c0], F32, name="raw%d" % len(loaded), align_bytes=64)
+            nc.sync.dma_start(out=raw[:], in_=source[:, c0:c1].rearrange("(p j) c -> p j c", j=PACK))
+            loaded.append((source is w, c0, c1, raw))
+
+        def load_g(t0, t1):
+            gt = keep.tile([P, t1 - t0, N], F32, name="g%d" % t0, align_bytes=64)
+            nc.sync.dma_start(out=gt[:], in_=g[P * t0 : P * t1, :].rearrange("(a p) n -> p a n", p=P))
+            for t in range(t0, t1):
+                gs[t] = gt[:, t - t0, :]
+
+        load_k(x, 0, 256)
+        load_k(x, 256, 512)
+        load_k(w, 0, 512)
+        load_k(x, 512, 1024)
+        load_g(0, 4)
+        load_k(x, 1024, 1536)
+        load_g(4, 8)
+        load_g(8, 12)
 
         def raw_cols(b, c0, c1):
-            for kind, d0, d1, raw in loaded:
-                if kind == b[0] and d0 <= W * b[1] + c0 and W * b[1] + c1 <= d1:
-                    s0 = W * b[1] + c0 - d0
-                    return raw[:, :, s0 : s0 + c1 - c0]
+            source, col, width = blocks[b]
+            for is_w, d0, d1, raw in loaded:
+                if is_w == (b == "w") and d0 <= col + c0 and col + c1 <= d1:
+                    return raw[:, :, col + c0 - d0 : col + c1 - d0]
             raise ValueError("columns not loaded in one piece")
-
-        def load_k(src, kind, c0, width):
-            raw = keep.tile([P, PACK, width], F32, name="r%s%d" % (kind, c0), align_bytes=64)
-            nc.sync.dma_start(out=raw[:], in_=src[:, c0 : c0 + width].rearrange("(p j) c -> p j c", j=PACK))
-            loaded.append((kind, c0, c0 + width, raw))
-
-        def load_g(t0, rows):
-            t = keep.tile([P, rows // P, N], F32, name="g%d" % t0, align_bytes=64)
-            nc.sync.dma_start(out=t[:], in_=g[t0 : t0 + rows, :].rearrange("(a p) n -> p a n", p=P))
-            for i in range(rows // P):
-                gs[t0 // P + i] = t[:, i, :]
-
-        load_k(x, "x", 0, 160)
-        load_k(x, "x", 160, 352)
-        load_k(w, "w", 0, 512)
-        load_k(x, "x", 512, 512)
-        load_g(0, 512)
-        load_k(x, "x", 1024, 512)
-        load_g(512, 512)
-        load_g(1024, 512)
-
-        blocks = [("x", 0), ("x", 1), ("w", 0), ("w", 1), ("x", 2), ("x", 3), ("x", 4), ("x", 5)]
-        codes, scales = {}, {}
-        for part in ("hi", "lo"):
-            codes["w", part] = keep.tile([P, N], U32, name="wc" + part, align_bytes=64)
-            scales["w", part] = keep.tile([P, N], U8, name="ws" + part, align_bytes=64)
-        top, hi, lo = {}, {}, {}
-        for b in blocks:
-            tag = "%s%d" % b
-            top[b] = keep.tile([P, W * PACK], BF16, name="top" + tag, align_bytes=64)
-            hi[b] = keep.tile([P, W * PACK], BF16, name="hi" + tag, align_bytes=64)
-            lo[b] = keep.tile([P, W * PACK], BF16, name="lo" + tag, align_bytes=64)
-            if b[0] == "x":
-                for part in ("hi", "lo"):
-                    codes[b, part] = keep.tile([P, W], U32, name="xc" + part + tag, align_bytes=64)
-                    scales[b, part] = keep.tile([P, W], U8, name="xs" + part + tag, align_bytes=64)
 
         def grouped(t, i, c0, c1):
             return t[:, PACK * c0 : PACK * c1].rearrange("p (c i j) -> p c j i", i=i, j=PACK)
 
-        def copy_top(b, c0=0, c1=W):
+        def copy_top(b, c0, c1):
             src = raw_cols(b, c0, c1).bitcast(BF16)[:, :, 1::2]
             nc.scalar.copy(out=grouped(top[b], 4, c0, c1), in_=src.rearrange("p j (c i) -> p c j i", i=4))
 
-        def mask(b, c0=0, c1=W):
+        def mask(b, c0, c1):
             nc.vector.tensor_scalar(
                 out=hi[b][:, PACK * c0 : PACK * c1].bitcast(I32),
                 in0=top[b][:, PACK * c0 : PACK * c1].bitcast(I32),
@@ -88,45 +80,47 @@ def tile_mix_split3_tm_mul_kernel(tc, w, x, g, out):
                 op0=ALU.bitwise_and,
             )
 
-        def sub(b, c0=0, c1=W, eng=None):
-            (nc.vector if eng is None else eng).tensor_tensor(
+        def sub(b, c0, c1, eng):
+            eng.tensor_tensor(
                 out=grouped(lo[b], 2, c0, c1),
                 in0=raw_cols(b, c0, c1).rearrange("p j (c i) -> p c j i", i=2),
                 in1=grouped(hi[b], 2, c0, c1),
                 op=ALU.subtract,
             )
 
-        def quant(b, part, c0=0, c1=W):
+        def quant(b, part, c0, c1):
             src = (hi if part == "hi" else lo)[b]
-            key, d0 = ("w", W * b[1]) if b[0] == "w" else (b, 0)
             nc.vector.quantize_mx(
-                out=codes[key, part][:, d0 + c0 : d0 + c1].bitcast(FP8X4),
-                scales=scales[key, part][:, d0 + c0 : d0 + c1],
+                out=codes[b, part][:, c0:c1].bitcast(FP8X4),
+                scales=scales[b, part][:, c0:c1],
                 in_=src[:, PACK * c0 : PACK * c1],
             )
 
+        block_of = ["xa", "xa", "xb", "xb"] + ["xc"] * 4 + ["xd"] * 4
         acc, outs = {}, {}
 
         def mm(t, xp, wp, start, stop):
-            cols = slice(128 * (t % 2), 128 * (t % 2) + 128)
-            b = ("x", t // 2)
+            b = block_of[t]
+            c0 = P * t - blocks[b][1]
             nc.tensor.matmul_mx(
                 out=acc[t][:],
-                lhsT=codes[b, xp][:, cols].bitcast(FP8X4),
-                lhsT_scale=scales[b, xp][:, cols],
+                lhsT=codes[b, xp][:, c0 : c0 + P].bitcast(FP8X4),
+                lhsT_scale=scales[b, xp][:, c0 : c0 + P],
                 rhs=codes["w", wp][:].bitcast(FP8X4),
                 rhs_scale=scales["w", wp][:],
                 start=start,
                 stop=stop,
             )
 
-        def mm_hi(t):
-            acc[t] = psum.tile([P, N], F32, name="acc")
-            mm(t, "hi", "hi", True, False)
-            mm(t, "hi", "lo", False, False)
+        def mm_hi(*tiles):
+            for t in tiles:
+                acc[t] = psum.tile([P, N], F32, name="acc")
+                mm(t, "hi", "hi", True, False)
+                mm(t, "hi", "lo", False, False)
 
-        def mm_lo(t):
-            mm(t, "lo", "hi", False, True)
+        def mm_lo(*tiles):
+            for t in tiles:
+                mm(t, "lo", "hi", False, True)
 
         def epi(t, n0=0, n1=N):
             if t // 2 not in outs:
@@ -139,56 +133,92 @@ def tile_mix_split3_tm_mul_kernel(tc, w, x, g, out):
             dst = out[P * t0 : P * t1, n0:n1].rearrange("(a p) n -> p a n", p=P)
             nc.sync.dma_start(out=dst, in_=outs[t0 // 2][:, t0 % 2 : t0 % 2 + t1 - t0, n0:n1])
 
-        pieces = ((0, 80), (80, 160), (160, 256))
-        first = blocks[0]
-        for c0, c1 in pieces:
-            copy_top(first, c0, c1)
-        for b in blocks[1:]:
-            copy_top(b)
-        for c0, c1 in pieces:
-            mask(first, c0, c1)
-            sub(first, c0, c1)
+        V, G = nc.vector, nc.gpsimd
+        for b, c0, c1 in (
+            ("xa", 0, 64), ("xa", 64, 160), ("xa", 160, 256),
+            ("xb", 0, 128), ("xb", 128, 256),
+            ("w", 0, 128), ("w", 128, 256), ("w", 256, 512),
+            ("xc", 0, 256), ("xc", 256, 512), ("xd", 0, 256), ("xd", 256, 512),
+        ):
+            copy_top(b, c0, c1)
 
-        gp = {("x", 3): 80, ("x", 4): 120, ("x", 5): 120}
-        epis = {("x", 2): (0, 1,), ("x", 3): (2, 3, 4,), ("x", 4): (5, 6, 7,)}
-        for b, following in zip(blocks, blocks[1:]):
-            if b not in epis:
-                quant(b, "hi")
-                if b != first:
-                    sub(b)
-                mask(following)
-                quant(b, "lo")
-            else:
-                sub(b, 0, W - gp.get(b, 0))
-                quant(b, "hi")
-                quant(b, "lo")
-                mask(following)
-                if following in gp:
-                    sub(following, W - gp[following], W, nc.gpsimd)
-            if b == ("w", 1):
-                for t in range(4):
-                    mm_hi(t)
-                    mm_lo(t)
-            if b[0] == "x" and b[1] >= 2:
-                for t in (2 * b[1], 2 * b[1] + 1):
-                    mm_hi(t)
-                for t in (2 * b[1], 2 * b[1] + 1):
-                    mm_lo(t)
-            for t in epis.get(b, ()):
-                epi(t)
-                if t % 2 == 1:
-                    store(t - 1, t + 1)
+        mask("xa", 0, 64)
+        mask("xa", 64, 160)
+        sub("xa", 0, 64, V)
+        mask("xa", 160, 256)
+        sub("xa", 64, 160, V)
+        quant("xa", "hi", 0, 256)
+        sub("xa", 160, 256, V)
+        mask("xb", 0, 128)
+        quant("xa", "lo", 0, 256)
 
-        b = blocks[-1]
-        quant(b, "hi")
-        mm_hi(10)
-        mm_hi(11)
-        sub(b, 0, W - gp.get(b, 0))
+        sub("xb", 0, 64, V)
+        mask("xb", 128, 256)
+        sub("xb", 64, 128, V)
+        quant("xb", "hi", 0, 256)
+        sub("xb", 128, 256, V)
+        mask("w", 0, 128)
+        quant("xb", "lo", 0, 256)
+
+        sub("w", 0, 64, V)
+        mask("w", 128, 256)
+        sub("w", 64, 128, V)
+        sub("w", 128, 192, V)
+        mask("w", 256, 512)
+        sub("w", 192, 256, V)
+        quant("w", "hi", 0, 512)
+        sub("w", 256, 512, V)
+        mask("xc", 0, 256)
+        quant("w", "lo", 0, 512)
+        for t in range(4):
+            mm_hi(t)
+            mm_lo(t)
+
+        sub("xc", 0, 256, V)
+        quant("xc", "hi", 0, 256)
+        quant("xc", "lo", 0, 256)
+        mask("xc", 256, 512)
+        sub("xc", 464, 512, G)
+        mm_hi(4, 5)
+        mm_lo(4, 5)
+        epi(0)
+        epi(1)
+        store(0, 2)
+
+        sub("xc", 256, 464, V)
+        quant("xc", "hi", 256, 512)
+        quant("xc", "lo", 256, 512)
+        mask("xd", 0, 256)
+        sub("xd", 160, 256, G)
+        mm_hi(6, 7)
+        mm_lo(6, 7)
+        epi(2)
+        epi(3)
+        store(2, 4)
+        epi(4)
+        store(4, 5)
+
+        sub("xd", 0, 160, V)
+        quant("xd", "hi", 0, 256)
+        quant("xd", "lo", 0, 256)
+        mask("xd", 256, 512)
+        sub("xd", 416, 512, G)
+        mm_hi(8, 9)
+        mm_lo(8, 9)
+        epi(5)
+        store(5, 6)
+        epi(6)
+        epi(7)
+        store(6, 8)
+
+        quant("xd", "hi", 256, 512)
+        mm_hi(10, 11)
+        sub("xd", 256, 416, V)
         epi(8)
         store(8, 9)
-        quant(b, "lo", 0, 128)
+        quant("xd", "lo", 256, 384)
         mm_lo(10)
-        quant(b, "lo", 128, 256)
+        quant("xd", "lo", 384, 512)
         mm_lo(11)
         epi(9)
         store(9, 10)

from contextlib import ExitStack

import concourse.mybir as mybir

K, N, T = 512, 512, 1536
FLOPS = 2 * K * N * T * 3

F32 = mybir.dt.float32
BF16 = mybir.dt.bfloat16
I32 = mybir.dt.int32
U32 = mybir.dt.uint32
U8 = mybir.dt.uint8
FP8X4 = mybir.dt.float8_e4m3fn_x4
ALU = mybir.AluOpType

P = 128
PACK = 4
MASK2 = -983056


def tile_mix_split3_tm_mul_kernel(tc, w, x, g, out):
    nc = tc.nc
    with ExitStack() as ctx:
        keep = ctx.enter_context(tc.tile_pool(name="keep", bufs=1))
        psum = ctx.enter_context(tc.psum_pool(name="psum", bufs=8))
        ctx.enter_context(tc.manual_schedule())

        blocks = {"xa": (x, 0, 256), "xb": (x, 256, 256), "w": (w, 0, 512), "xc": (x, 512, 512), "xd": (x, 1024, 512)}
        top, hi, lo, codes, scales = {}, {}, {}, {}, {}
        for b, (source, col, width) in blocks.items():
            top[b] = keep.tile([P, width * PACK], BF16, name="top_" + b, align_bytes=64)
            hi[b] = keep.tile([P, width * PACK], BF16, name="hi_" + b, align_bytes=64)
            lo[b] = keep.tile([P, width * PACK], BF16, name="lo_" + b, align_bytes=64)
            for part in ("hi", "lo"):
                codes[b, part] = keep.tile([P, width], U32, name="codes_%s_%s" % (part, b), align_bytes=64)
                scales[b, part] = keep.tile([P, width], U8, name="scales_%s_%s" % (part, b), align_bytes=64)

        loaded, gs = [], {}

        def load_k(source, c0, c1):
            raw = keep.tile([P, PACK, c1 - c0], F32, name="raw%d" % len(loaded), align_bytes=64)
            nc.sync.dma_start(out=raw[:], in_=source[:, c0:c1].rearrange("(p j) c -> p j c", j=PACK))
            loaded.append((source is w, c0, c1, raw))

        def load_g(t0, t1):
            gt = keep.tile([P, t1 - t0, N], F32, name="g%d" % t0, align_bytes=64)
            nc.sync.dma_start(out=gt[:], in_=g[P * t0 : P * t1, :].rearrange("(a p) n -> p a n", p=P))
            for t in range(t0, t1):
                gs[t] = gt[:, t - t0, :]

        load_k(x, 0, 256)
        load_k(x, 256, 512)
        load_k(w, 0, 512)
        load_k(x, 512, 1024)
        load_g(0, 4)
        load_k(x, 1024, 1536)
        load_g(4, 8)
        load_g(8, 12)

        def raw_cols(b, c0, c1):
            source, col, width = blocks[b]
            for is_w, d0, d1, raw in loaded:
                if is_w == (b == "w") and d0 <= col + c0 and col + c1 <= d1:
                    return raw[:, :, col + c0 - d0 : col + c1 - d0]
            raise ValueError("columns not loaded in one piece")

        def grouped(t, i, c0, c1):
            return t[:, PACK * c0 : PACK * c1].rearrange("p (c i j) -> p c j i", i=i, j=PACK)

        def copy_top(b, c0, c1):
            src = raw_cols(b, c0, c1).bitcast(BF16)[:, :, 1::2]
            nc.scalar.copy(out=grouped(top[b], 4, c0, c1), in_=src.rearrange("p j (c i) -> p c j i", i=4))

        def mask(b, c0, c1):
            nc.vector.tensor_scalar(
                out=hi[b][:, PACK * c0 : PACK * c1].bitcast(I32),
                in0=top[b][:, PACK * c0 : PACK * c1].bitcast(I32),
                scalar1=MASK2,
                scalar2=None,
                op0=ALU.bitwise_and,
            )

        def sub(b, c0, c1, eng):
            eng.tensor_tensor(
                out=grouped(lo[b], 2, c0, c1),
                in0=raw_cols(b, c0, c1).rearrange("p j (c i) -> p c j i", i=2),
                in1=grouped(hi[b], 2, c0, c1),
                op=ALU.subtract,
            )

        def quant(b, part, c0, c1):
            src = (hi if part == "hi" else lo)[b]
            nc.vector.quantize_mx(
                out=codes[b, part][:, c0:c1].bitcast(FP8X4),
                scales=scales[b, part][:, c0:c1],
                in_=src[:, PACK * c0 : PACK * c1],
            )

        block_of = ["xa", "xa", "xb", "xb"] + ["xc"] * 4 + ["xd"] * 4
        acc, outs = {}, {}

        def mm(t, xp, wp, start, stop):
            b = block_of[t]
            c0 = P * t - blocks[b][1]
            nc.tensor.matmul_mx(
                out=acc[t][:],
                lhsT=codes[b, xp][:, c0 : c0 + P].bitcast(FP8X4),
                lhsT_scale=scales[b, xp][:, c0 : c0 + P],
                rhs=codes["w", wp][:].bitcast(FP8X4),
                rhs_scale=scales["w", wp][:],
                start=start,
                stop=stop,
            )

        def mm_hi(*tiles):
            for t in tiles:
                acc[t] = psum.tile([P, N], F32, name="acc")
                mm(t, "hi", "hi", True, False)
                mm(t, "hi", "lo", False, False)

        def mm_lo(*tiles):
            for t in tiles:
                mm(t, "lo", "hi", False, True)

        def epi(t, n0=0, n1=N):
            if t // 2 not in outs:
                outs[t // 2] = keep.tile([P, 2, N], F32, name="o%d" % (t // 2), align_bytes=64)
            nc.vector.tensor_tensor(
                out=outs[t // 2][:, t % 2, n0:n1], in0=acc[t][:, n0:n1], in1=gs[t][:, n0:n1], op=ALU.mult
            )

        def store(t0, t1, n0=0, n1=N):
            dst = out[P * t0 : P * t1, n0:n1].rearrange("(a p) n -> p a n", p=P)
            nc.sync.dma_start(out=dst, in_=outs[t0 // 2][:, t0 % 2 : t0 % 2 + t1 - t0, n0:n1])

        V, G = nc.vector, nc.gpsimd
        for b, c0, c1 in (
            ("xa", 0, 64), ("xa", 64, 160), ("xa", 160, 256),
            ("xb", 0, 128), ("xb", 128, 256),
            ("w", 0, 128), ("w", 128, 256), ("w", 256, 512),
            ("xc", 0, 256), ("xc", 256, 512), ("xd", 0, 256), ("xd", 256, 512),
        ):
            copy_top(b, c0, c1)

        mask("xa", 0, 64)
        mask("xa", 64, 160)
        sub("xa", 0, 64, V)
        mask("xa", 160, 256)
        sub("xa", 64, 160, V)
        quant("xa", "hi", 0, 256)
        sub("xa", 160, 256, V)
        mask("xb", 0, 128)
        quant("xa", "lo", 0, 256)

        sub("xb", 0, 64, V)
        mask("xb", 128, 256)
        sub("xb", 64, 128, V)
        quant("xb", "hi", 0, 256)
        sub("xb", 128, 256, V)
        mask("w", 0, 128)
        quant("xb", "lo", 0, 256)

        sub("w", 0, 64, V)
        mask("w", 128, 256)
        sub("w", 64, 128, V)
        sub("w", 128, 192, V)
        mask("w", 256, 512)
        sub("w", 192, 256, V)
        quant("w", "hi", 0, 512)
        sub("w", 256, 512, V)
        mask("xc", 0, 256)
        quant("w", "lo", 0, 512)
        for t in range(4):
            mm_hi(t)
            mm_lo(t)

        sub("xc", 0, 256, V)
        quant("xc", "hi", 0, 256)
        quant("xc", "lo", 0, 256)
        mask("xc", 256, 512)
        sub("xc", 464, 512, G)
        mm_hi(4, 5)
        mm_lo(4, 5)
        epi(0)
        epi(1)
        store(0, 2)

        sub("xc", 256, 464, V)
        quant("xc", "hi", 256, 512)
        quant("xc", "lo", 256, 512)
        mask("xd", 0, 256)
        sub("xd", 160, 256, G)
        mm_hi(6, 7)
        mm_lo(6, 7)
        epi(2)
        epi(3)
        store(2, 4)
        epi(4)
        store(4, 5)

        sub("xd", 0, 160, V)
        quant("xd", "hi", 0, 256)
        quant("xd", "lo", 0, 256)
        mask("xd", 256, 512)
        sub("xd", 416, 512, G)
        mm_hi(8, 9)
        mm_lo(8, 9)
        epi(5)
        store(5, 6)
        epi(6)
        epi(7)
        store(6, 8)

        quant("xd", "hi", 256, 512)
        mm_hi(10, 11)
        sub("xd", 256, 416, V)
        epi(8)
        store(8, 9)
        quant("xd", "lo", 256, 384)
        mm_lo(10)
        quant("xd", "lo", 384, 512)
        mm_lo(11)
        epi(9)
        store(9, 10)
        epi(10)
        store(10, 11)
        for n0 in (0, 256):
            epi(11, n0, n0 + 256)
            store(11, 12, n0, n0 + 256)
